import numpy as np
import ml_dtypes


def mxq(x, axis, fmt="e4m3"):
    dtype, down = {"e4m3": (ml_dtypes.float8_e4m3fn, 7), "e5m2": (ml_dtypes.float8_e5m2, 14)}[fmt]
    v = np.moveaxis(np.asarray(x, np.float32).astype(ml_dtypes.bfloat16).astype(np.float64), axis, -1)
    blocks = v.reshape(v.shape[:-1] + (-1, 32))
    amax = np.abs(blocks).max(-1, keepdims=True)
    byte = np.maximum(np.where(amax > 0, np.frexp(amax)[1] - 1 + 127, 0) - down, 1)
    scale = np.exp2(byte - 127.0)
    codes = (blocks / scale).astype(np.float32).astype(dtype).astype(np.float64)
    return np.moveaxis((codes * scale).reshape(v.shape), -1, axis)


WIDE = False


def mx_kscale(k):
    if not WIDE:
        return np.ones(k)
    levels = np.array([10, -10, 5, -5, 0])
    if k % 512:
        return np.exp2(np.random.permutation(np.resize(levels, k // 32))).repeat(32)
    a = np.empty((k // 512, 16))
    for p in range(k // 512):
        a[p, :8] = np.random.permutation(np.resize(levels, 8))
        for g in range(8):
            far = levels[np.abs(levels - a[p, g]) >= 10]
            a[p, g + 8] = far[np.random.randint(len(far))]
    return np.exp2(a.ravel()).repeat(32)


def f64(x):
    return np.asarray(x).astype(np.float64)


def striped(idx):
    return np.tile(np.asarray(idx).reshape(-1, 16).T, (8, 1)).astype(np.uint16)


def unstriped(offs):
    return offs[:16].T.reshape(-1).astype(np.int64)


E2M1 = np.array([0.0, 0.5, 1.0, 1.5, 2.0, 3.0, 4.0, 6.0, -0.0, -0.5, -1.0, -1.5, -2.0, -3.0, -4.0, -6.0])


def pack_weight(w, fmt):
    k, n = w.shape
    w = f64(np.asarray(w, np.float32).astype(ml_dtypes.bfloat16)).reshape(k // 32, 32, n)
    amax = np.abs(w).max(1)
    if fmt == "e4m3":
        byte = np.frexp(amax)[1] - 1 + 127 - 7
    else:
        mant, ex = np.frexp(amax / 6.0)
        byte = np.where(mant > 0.5, ex, ex - 1) + 127
    byte = np.clip(np.where(amax > 0, byte, 1), 1, 254)
    scaled = (w * np.exp2(127.0 - byte)[:, None, :]).reshape(k, n).astype(np.float32)
    by_word = np.ascontiguousarray(scaled.reshape(k // 512, 128, 4, n).transpose(0, 1, 3, 2))
    if fmt == "e4m3":
        words = by_word.astype(ml_dtypes.float8_e4m3fn).view(np.uint8)
    else:
        c = by_word.astype(ml_dtypes.float4_e2m1fn).view(np.uint8) & 0xF
        words = (c[..., 0::2] | (c[..., 1::2] << 4)).reshape(k // 512, 128, 2 * n)
    return np.ascontiguousarray(words), np.ascontiguousarray(byte.astype(np.uint8).reshape(k // 512, 16, n))


def unpack_weight(words, scales, fmt):
    g, _, n = scales.shape
    words = np.ascontiguousarray(words).reshape(g, 128, n, -1)
    if fmt == "e4m3":
        vals = words.view(ml_dtypes.float8_e4m3fn).astype(np.float64)
    else:
        nib = np.empty((g, 128, n, 4), np.uint8)
        nib[..., 0::2] = words & 0xF
        nib[..., 1::2] = words >> 4
        vals = E2M1[nib]
    vals = vals * np.repeat(np.exp2(scales.astype(np.float64) - 127.0), 8, axis=1)[..., None]
    return vals.transpose(0, 1, 3, 2).reshape(g * 512, n)


def bf(x):
    return np.asarray(x, np.float32).astype(ml_dtypes.bfloat16)


def planes(Y):
    r, m = Y.shape
    b = f64(bf(Y)).reshape(r // 32, 32, m)
    amax = np.abs(b).max(1)
    byte = np.clip(np.where(amax > 0, np.frexp(amax)[1] - 1 + 127 - 7, 1), 1, 254)
    codes = (b * np.exp2(127.0 - byte)[:, None, :]).reshape(r, m).astype(np.float32).astype(ml_dtypes.float8_e4m3fn).view(np.uint8)
    words = codes.reshape(r // 512, 128, 4, m).transpose(0, 1, 3, 2)
    return np.ascontiguousarray(words), np.ascontiguousarray(byte.astype(np.uint8).reshape(r // 512, 16, m))


K, S, T, N = 1024, 512, 512, 512


def setup_inputs():
    n = np.random.standard_normal
    idx = np.random.randint(0, S, T)
    idx2 = np.random.randint(0, S, T)
    fk = mx_kscale(K)
    wap = pack_weight(n((K, N)) * 1 / np.sqrt(K) * fk[:, None], "e2m1")
    return {
        "xb": (n((K, S)) / fk[:, None]).astype(np.float32),
        "wa_words": wap[0],
        "wa_scales": wap[1],
        "ga": (np.random.uniform(0.4, 1.0, (1, T))).astype(np.float32),
        "offs": striped(idx),
        "offs2": striped(idx2),
    }


def reference(xb, wa_words, wa_scales, ga, offs, offs2):
    idx = unstriped(offs)
    idx2 = unstriped(offs2)
    wau = unpack_weight(wa_words, wa_scales, "e2m1")
    xbq = mxq(f64(xb), 0, "e4m3")
    z = wau.T @ xbq
    y = f64(ga) * z[:, idx] / (1.0 + np.abs(z[:, idx] - z[:, idx2]))
    words, scales = planes(y)
    return y, words, scales

@@ -1,0 +1,247 @@
+from contextlib import ExitStack
+
+import concourse.mybir as mybir
+from concourse.masks import make_identity
+
+K, S, T, N = 1024, 512, 512, 512
+FLOPS = 2 * K * S * N
+
+F32 = mybir.dt.float32
+BF16 = mybir.dt.bfloat16
+I32 = mybir.dt.int32
+U32 = mybir.dt.uint32
+U16 = mybir.dt.uint16
+U8 = mybir.dt.uint8
+FP8X4 = mybir.dt.float8_e4m3fn_x4
+FP4X4 = mybir.dt.float4_e2m1fn_x4
+ALU = mybir.AluOpType
+ACT = mybir.ActivationFunctionType
+
+P = 128
+PACK = 4
+PASSES = K // (P * PACK)
+QUARTER = 128
+
+X_PIECES = ((0, 0, 256, 160), (0, 256, 256, 160), (1, 0, 256, 160), (1, 256, 128, 80), (1, 384, 128, 80))
+CHUNK = 128
+CHUNKS = T // CHUNK
+LARGEST = 3.0e38
+
+
+def tile_moe_buffer_read_with_doubt_pl_kernel(tc, xb, wa_words, wa_scales, ga, offs, offs2, out_0, out_1, out_2):
+    nc = tc.nc
+    with ExitStack() as ctx:
+        keep = ctx.enter_context(tc.tile_pool(name="keep", bufs=1))
+        psum = ctx.enter_context(tc.psum_pool(name="psum", bufs=1))
+
+        unit = keep.tile([P, 1], F32, name="unit")
+        one = keep.tile([P, 1], F32, name="one")
+        nc.gpsimd.memset(unit[:], 1.0)
+        nc.scalar.activation(one[:], unit[:], ACT.Abs_reciprocal_sqrt)
+
+        w_raw = keep.tile([P, PASSES * 2 * N], U8, name="w_raw", align_bytes=64)
+        ws_raw = keep.tile([P, PASSES * N], U8, name="ws_raw", align_bytes=64)
+        nc.vector.memset(ws_raw[:].bitcast(I32), 0)
+
+        x_rows = xb.rearrange("(g p j) s -> g p j s", g=PASSES, j=PACK)
+        x_raw = []
+
+        def load_x(i):
+            g, s0, width, on_vector = X_PIECES[i]
+            raw = keep.tile([P, PACK, width], F32, name="x_raw%d" % i)
+            nc.sync.dma_start(raw[:], x_rows[g][:, :, s0 : s0 + width])
+            x_raw.append(raw)
+
+        identity = keep.tile([P, P], F32, name="identity")
+        make_identity(nc, identity[:])
+        ga_rows = keep.tile([P, P], F32, name="ga_rows")
+        nc.gpsimd.memset(ga_rows[:], 0.0)
+
+        def bank(b, name):
+            return psum.tile([P, PACK, P], F32, name=name, tag="bank%d" % b)
+
+        load_x(0)
+        nc.sync.dma_start(ga_rows[0:CHUNKS, :], ga[0].rearrange("(c p) -> c p", p=CHUNK))
+        nc.sync.dma_start(
+            w_raw[:].bitcast(I32).rearrange("p (g b) -> p g b", g=PASSES),
+            wa_words.bitcast(I32).rearrange("g p b -> p g b"),
+        )
+        for q in range(4):
+            nc.sync.dma_start(
+                ws_raw[32 * q : 32 * q + 4, :].bitcast(I32).rearrange("p (g b) -> p g b", g=PASSES),
+                wa_scales.bitcast(I32).rearrange("g r b -> r g b")[4 * q : 4 * q + 4],
+            )
+        for i in range(1, len(X_PIECES)):
+            load_x(i)
+        first = keep.tile([P, T // 16], U16, name="first")
+        second = keep.tile([P, T // 16], U16, name="second")
+        nc.sync.dma_start(first[:], offs)
+        nc.sync.dma_start(second[:], offs2)
+
+        turned = bank(0, "turned")
+        nc.tensor.transpose(turned[:, 0, :], ga_rows[:], identity[:])
+        ga_cols = keep.tile([P, CHUNKS], F32, name="ga_cols")
+        nc.scalar.copy(ga_cols[:], turned[:, 0, 0:CHUNKS])
+        spread = bank(7, "spread")
+        for c in range(CHUNKS):
+            nc.tensor.transpose(spread[:, c, :], ga_cols[:, c : c + 1].to_broadcast([P, P]), identity[:])
+        gate = keep.tile([P, T], F32, name="gate")
+        minus_gate = keep.tile([P, T], F32, name="minus_gate")
+        nc.scalar.copy(gate[:], spread[:].rearrange("p c t -> p (c t)"))
+        nc.scalar.activation(minus_gate[:], spread[:].rearrange("p c t -> p (c t)"), ACT.Copy, scale=-1.0)
+        nonzero = keep.tile([P, CHUNKS], F32, name="nonzero")
+        inverse_raw = keep.tile([P, CHUNKS], F32, name="inverse_raw")
+        inverse = keep.tile([P, CHUNKS], F32, name="inverse")
+        nc.vector.scalar_tensor_tensor(nonzero[:], ga_cols[:], 0.0, ga_cols[:], ALU.is_equal, ALU.add)
+        nc.vector.reciprocal(inverse_raw[:], nonzero[:])
+        nc.vector.tensor_scalar(inverse[:], inverse_raw[:], LARGEST, -LARGEST, ALU.min, ALU.max)
+
+        w = keep.tile([P, PASSES * 2 * N], U8, name="w", align_bytes=64)
+        ws = keep.tile([P, PASSES * N], U8, name="ws", align_bytes=64)
+        nc.vector.tensor_copy(
+            w[:].bitcast(U16).rearrange("p (g j m) -> p g j m", g=PASSES, j=PACK),
+            w_raw[:].bitcast(U16).rearrange("p (g m j) -> p g j m", g=PASSES, j=PACK),
+        )
+        nc.vector.tensor_copy(
+            ws[:].rearrange("p (g j m) -> p g j m", g=PASSES, j=PACK),
+            ws_raw[:].rearrange("p (g m j) -> p g j m", g=PASSES, j=PACK),
+        )
+
+        x_codes = {}
+
+        def quantize_x(i):
+            g, s0, width, on_vector = X_PIECES[i]
+            grouped = keep.tile([P, width * PACK], BF16, name="x_bf%d" % i, align_bytes=64)
+            dst = grouped[:].rearrange("p (c i j) -> p c j i", i=4, j=PACK)
+            src = x_raw[i][:].rearrange("p j (c i) -> p c j i", i=4)
+            cut = on_vector // 4
+            nc.scalar.copy(dst[:, cut:], src[:, cut:])
+            nc.vector.tensor_copy(dst[:, :cut], src[:, :cut])
+            codes = keep.tile([P, width], U32, name="x_codes%d" % i, align_bytes=64)
+            scales = keep.tile([P, width], U8, name="x_scales%d" % i, align_bytes=64)
+            nc.vector.quantize_mx(out=codes[:].bitcast(FP8X4), scales=scales[:], in_=grouped[:])
+            for a in range(width // QUARTER):
+                cols = slice(a * QUARTER, (a + 1) * QUARTER)
+                x_codes[(g, s0 // QUARTER + a)] = (codes[:, cols], scales[:, cols])
+
+        def product(out, j, quarter, g):
+            codes, scales = x_codes[(g, quarter)]
+            block = g * PACK + j
+            nc.tensor.matmul_mx(
+                out=out,
+                lhsT=w[:, block * 2 * P : (block + 1) * 2 * P].bitcast(FP4X4),
+                lhsT_scale=ws[:, block * P : (block + 1) * P],
+                rhs=codes.bitcast(FP8X4),
+                rhs_scale=scales,
+                start=(g == 0),
+                stop=(g == PASSES - 1),
+            )
+
+        z = [keep.tile([P, S], F32, name="z%d" % j) for j in range(PACK)]
+        last = S // QUARTER - 1
+        last_banks = [bank(3 + j, "last_bank%d" % j)[:, 0, :] for j in range(PACK)]
+
+        def early_quarter(quarter):
+            sums = bank(quarter, "sums%d" % quarter)
+            for j in range(PACK):
+                for g in range(PASSES):
+                    product(sums[:, j, :], j, quarter, g)
+            for j in range(PACK):
+                nc.scalar.copy(z[j][:, quarter * QUARTER : (quarter + 1) * QUARTER], sums[:, j, :])
+
+        quantize_x(0)
+        quantize_x(1)
+        for j in range(PACK):
+            product(last_banks[j], j, last, 0)
+        quantize_x(2)
+        early_quarter(0)
+        quantize_x(3)
+        early_quarter(1)
+        quantize_x(4)
+        early_quarter(2)
+        for j in range(PACK):
+            product(last_banks[j], j, last, 1)
+            nc.scalar.copy(z[j][:, last * QUARTER :], last_banks[j])
+
+        y_codes = keep.tile([P, T], U32, name="y_codes", align_bytes=64)
+        y_scales = keep.tile([P, T], U8, name="y_scales", align_bytes=64)
+        out_rows = out_0.rearrange("(p j) t -> p j t", j=PACK)
+        out_words = out_1[0].rearrange("p c r -> p (c r)").bitcast(I32)
+        made = {}
+
+        banks_used = []
+
+        def next_bank(name):
+            order = (0, 1, 2, 7, 3, 4, 5, 6)
+            banks_used.append(name)
+            return bank(order[(len(banks_used) - 1) % 8], name)
+
+        def look_up(c, rows):
+            tokens = slice(c * CHUNK, (c + 1) * CHUNK)
+            entries = slice(c * CHUNK // 16, (c + 1) * CHUNK // 16)
+            n = len(rows)
+            key = "%d_%d" % (c, rows[0])
+            chosen = keep.tile([P, n, CHUNK], F32, name="chosen" + key)
+            other = keep.tile([P, n, CHUNK], F32, name="other" + key)
+            gap = next_bank("gap" + key)
+            for i, j in enumerate(rows):
+                nc.vector.tensor_tensor(chosen[:, i, :], z[j][:].indirect(first[:, entries]), gate[:, tokens], ALU.mult)
+                nc.vector.tensor_tensor(other[:, i, :], z[j][:].indirect(second[:, entries]), minus_gate[:, tokens], ALU.mult)
+                nc.tensor.matmul(gap[:, i, :], chosen[:, i, :], identity[:], is_transpose=True, start=True, stop=False)
+                nc.tensor.matmul(gap[:, i, :], other[:, i, :], identity[:], is_transpose=True, start=False, stop=True)
+            size = keep.tile([P, n, CHUNK], F32, name="size" + key)
+            root = keep.tile([P, n, CHUNK], F32, name="root" + key)
+            trust = keep.tile([P, n, CHUNK], F32, name="trust" + key)
+            nc.scalar.activation(size[:], gap[:, 0:n, :], ACT.Abs, scale=inverse[:, c : c + 1])
+            nc.scalar.activation(root[:], size[:], ACT.Abs_reciprocal_sqrt, bias=one[:])
+            nc.scalar.activation(trust[:], root[:], ACT.Square)
+            back = next_bank("back" + key)
+            for i in range(n):
+                nc.tensor.transpose(back[:, i, :], trust[:, i, :], identity[:])
+            made[(c, rows)] = (chosen, back)
+
+        y = [keep.tile([P, PACK, CHUNK], F32, name="y%d" % c) for c in range(CHUNKS)]
+        grouped = [keep.tile([P, CHUNK * PACK], BF16, name="y_bf%d" % c, align_bytes=64) for c in range(CHUNKS)]
+
+        def weigh(c, rows):
+            chosen, back = made[(c, rows)]
+            nc.vector.tensor_tensor(y[c][:, rows[0] : rows[-1] + 1, :], back[:, 0 : len(rows), :], chosen[:], ALU.mult)
+
+        def finish(c):
+            nc.sync.dma_start(out_rows[:, :, c * CHUNK : (c + 1) * CHUNK], y[c][:])
+            dst = grouped[c][:].rearrange("p (c i j) -> p c j i", i=4, j=PACK)
+            src = y[c][:].rearrange("p j (c i) -> p c j i", i=4)
+            if c == CHUNKS - 1:
+                nc.vector.tensor_copy(dst, src)
+            else:
+                nc.scalar.copy(dst, src)
+
+        def pack(c):
+            cols = slice(c * CHUNK, (c + 1) * CHUNK)
+            nc.vector.quantize_mx(out=y_codes[:, cols].bitcast(FP8X4), scales=y_scales[:, cols], in_=grouped[c][:])
+
+        whole, low, high = (0, 1, 2, 3), (0, 1), (2, 3)
+        look_up(0, whole)
+        look_up(1, whole)
+        look_up(2, whole)
+        weigh(0, whole)
+        finish(0)
+        look_up(3, low)
+        look_up(3, high)
+        weigh(1, whole)
+        finish(1)
+        pack(0)
+        weigh(2, whole)
+        finish(2)
+        pack(1)
+        weigh(3, low)
+        pack(2)
+        done = (CHUNKS - 1) * CHUNK
+        nc.sync.dma_start(out_words[:, :done], y_codes[:, :done].bitcast(I32))
+        weigh(3, high)
+        finish(3)
+        pack(3)
+        nc.sync.dma_start(out_words[:, done:], y_codes[:, done:].bitcast(I32))
+        for q in range(4):
+            queue = nc.scalar if q % 2 == 0 else nc.sync
+            queue.dma_start(out_2[0].bitcast(I32)[4 * q : 4 * q + 4, :], y_scales[32 * q : 32 * q + 4, :].bitcast(I32))

@@ -22,9 +22,11 @@ PACK = 4
 PASSES = K // (P * PACK)
 QUARTER = 128
 
-X_PIECES = ((0, 0, 256, 160), (0, 256, 256, 160), (1, 0, 256, 160), (1, 256, 128, 80), (1, 384, 128, 80))
+X_PIECES = ((0, 0, 256, 160), (1, 0, 256, 160), (0, 256, 256, 256), (1, 256, 128, 128), (1, 384, 128, 128))
+SPARE = 32
 CHUNK = 128
 CHUNKS = T // CHUNK
+HALF = T // 2
 LARGEST = 3.0e38
 
 
@@ -34,14 +36,13 @@ def tile_moe_buffer_read_with_doubt_pl_kernel(tc, xb, wa_words, wa_scales, ga, o
         keep = ctx.enter_context(tc.tile_pool(name="keep", bufs=1))
         psum = ctx.enter_context(tc.psum_pool(name="psum", bufs=1))
 
+        w_raw = keep.tile([P, PASSES * 2 * N], U8, name="w_raw", align_bytes=64)
+        ws_raw = keep.tile([P, PASSES * N], U8, name="ws_raw", align_bytes=64)
+        nc.gpsimd.memset(ws_raw[:].bitcast(I32), 0)
         unit = keep.tile([P, 1], F32, name="unit")
         one = keep.tile([P, 1], F32, name="one")
         nc.gpsimd.memset(unit[:], 1.0)
         nc.scalar.activation(one[:], unit[:], ACT.Abs_reciprocal_sqrt)
-
-        w_raw = keep.tile([P, PASSES * 2 * N], U8, name="w_raw", align_bytes=64)
-        ws_raw = keep.tile([P, PASSES * N], U8, name="ws_raw", align_bytes=64)
-        nc.vector.memset(ws_raw[:].bitcast(I32), 0)
 
         x_rows = xb.rearrange("(g p j) s -> g p j s", g=PASSES, j=PACK)
         x_raw = []
@@ -54,14 +55,14 @@ def tile_moe_buffer_read_with_doubt_pl_kernel(tc, xb, wa_words, wa_scales, ga, o
 
         identity = keep.tile([P, P], F32, name="identity")
         make_identity(nc, identity[:])
-        ga_rows = keep.tile([P, P], F32, name="ga_rows")
-        nc.gpsimd.memset(ga_rows[:], 0.0)
 
         def bank(b, name):
             return psum.tile([P, PACK, P], F32, name=name, tag="bank%d" % b)
 
         load_x(0)
-        nc.sync.dma_start(ga_rows[0:CHUNKS, :], ga[0].rearrange("(c p) -> c p", p=CHUNK))
+        ga_cols = keep.tile([P, CHUNKS], F32, name="ga_cols")
+        with nc.allow_non_contiguous_dma(reason="one gate value for each partition and block of tokens"):
+            nc.sync.dma_start(ga_cols[:], ga[0].rearrange("(c p) -> p c", p=CHUNK))
         nc.sync.dma_start(
             w_raw[:].bitcast(I32).rearrange("p (g b) -> p g b", g=PASSES),
             wa_words.bitcast(I32).rearrange("g p b -> p g b"),
@@ -78,17 +79,14 @@ def tile_moe_buffer_read_with_doubt_pl_kernel(tc, xb, wa_words, wa_scales, ga, o
         nc.sync.dma_start(first[:], offs)
         nc.sync.dma_start(second[:], offs2)
 
-        turned = bank(0, "turned")
-        nc.tensor.transpose(turned[:, 0, :], ga_rows[:], identity[:])
-        ga_cols = keep.tile([P, CHUNKS], F32, name="ga_cols")
-        nc.scalar.copy(ga_cols[:], turned[:, 0, 0:CHUNKS])
-        spread = bank(7, "spread")
-        for c in range(CHUNKS):
-            nc.tensor.transpose(spread[:, c, :], ga_cols[:, c : c + 1].to_broadcast([P, P]), identity[:])
+        sum_banks = (0, 2, 3, 4)
         gate = keep.tile([P, T], F32, name="gate")
         minus_gate = keep.tile([P, T], F32, name="minus_gate")
-        nc.scalar.copy(gate[:], spread[:].rearrange("p c t -> p (c t)"))
-        nc.scalar.activation(minus_gate[:], spread[:].rearrange("p c t -> p (c t)"), ACT.Copy, scale=-1.0)
+        for c in range(CHUNKS):
+            spread = bank(sum_banks[c], "spread%d" % c)
+            nc.tensor.transpose(spread[:, 0, :], ga_cols[:, c : c + 1].to_broadcast([P, P]), identity[:])
+            nc.scalar.copy(gate[:, c * CHUNK : (c + 1) * CHUNK], spread[:, 0, :])
+        nc.scalar.activation(minus_gate[:], gate[:], ACT.Copy, scale=-1.0)
         nonzero = keep.tile([P, CHUNKS], F32, name="nonzero")
         inverse_raw = keep.tile([P, CHUNKS], F32, name="inverse_raw")
         inverse = keep.tile([P, CHUNKS], F32, name="inverse")
@@ -115,7 +113,8 @@ def tile_moe_buffer_read_with_doubt_pl_kernel(tc, xb, wa_words, wa_scales, ga, o
             dst = grouped[:].rearrange("p (c i j) -> p c j i", i=4, j=PACK)
             src = x_raw[i][:].rearrange("p j (c i) -> p c j i", i=4)
             cut = on_vector // 4
-            nc.scalar.copy(dst[:, cut:], src[:, cut:])
+            if on_vector < width:
+                nc.scalar.copy(dst[:, cut:], src[:, cut:])
             nc.vector.tensor_copy(dst[:, :cut], src[:, :cut])
             codes = keep.tile([P, width], U32, name="x_codes%d" % i, align_bytes=64)
             scales = keep.tile([P, width], U8, name="x_scales%d" % i, align_bytes=64)
@@ -137,31 +136,39 @@ def tile_moe_buffer_read_with_doubt_pl_kernel(tc, xb, wa_words, wa_scales, ga, o
                 stop=(g == PASSES - 1),
             )
 
-        z = [keep.tile([P, S], F32, name="z%d" % j) for j in range(PACK)]
+        z = [keep.tile([P, S + SPARE], F32, name="z%d" % j) for j in range(PACK)]
+        for j in range(PACK):
+            nc.gpsimd.memset(z[j][:, S:], 0.0)
         last = S // QUARTER - 1
-        last_banks = [bank(3 + j, "last_bank%d" % j)[:, 0, :] for j in range(PACK)]
+        sums = [bank(sum_banks[j], "sums%d" % j) for j in range(PACK)]
+        last_sums = bank(1, "last_sums")
 
-        def early_quarter(quarter):
-            sums = bank(quarter, "sums%d" % quarter)
-            for j in range(PACK):
+        def products(quarter, rows):
+            for j in rows:
                 for g in range(PASSES):
-                    product(sums[:, j, :], j, quarter, g)
-            for j in range(PACK):
-                nc.scalar.copy(z[j][:, quarter * QUARTER : (quarter + 1) * QUARTER], sums[:, j, :])
+                    product(sums[j][:, quarter, :], j, quarter, g)
 
         quantize_x(0)
         quantize_x(1)
-        for j in range(PACK):
-            product(last_banks[j], j, last, 0)
+        products(0, (0,))
+        products(1, (0,))
         quantize_x(2)
-        early_quarter(0)
+        product(last_sums[:, 0, :], 0, last, 0)
         quantize_x(3)
-        early_quarter(1)
+        products(2, (0,))
+        nc.scalar.copy(z[0][:, : last * QUARTER], sums[0][:, 0:last, :].rearrange("p q s -> p (q s)"))
         quantize_x(4)
-        early_quarter(2)
-        for j in range(PACK):
-            product(last_banks[j], j, last, 1)
-            nc.scalar.copy(z[j][:, last * QUARTER :], last_banks[j])
+        product(last_sums[:, 0, :], 0, last, 1)
+        nc.scalar.copy(z[0][:, last * QUARTER : S], last_sums[:, 0, :])
+        for j in range(1, PACK):
+            for quarter in (0, 1):
+                products(quarter, (j,))
+            late_sums = bank(1, "late_sums%d" % j)
+            for quarter in (2, 3):
+                for g in range(PASSES):
+                    product(late_sums[:, quarter, :], j, quarter, g)
+            nc.scalar.copy(z[j][:, : S // 2], sums[j][:, 0:2, :].rearrange("p q s -> p (q s)"))
+            nc.scalar.copy(z[j][:, S // 2 : S], late_sums[:, 2:4, :].rearrange("p q s -> p (q s)"))
 
         y_codes = keep.tile([P, T], U32, name="y_codes", align_bytes=64)
         y_scales = keep.tile([P, T], U8, name="y_scales", align_bytes=64)
@@ -169,79 +176,80 @@ def tile_moe_buffer_read_with_doubt_pl_kernel(tc, xb, wa_words, wa_scales, ga, o
         out_words = out_1[0].rearrange("p c r -> p (c r)").bitcast(I32)
         made = {}
 
-        banks_used = []
+        y_all = keep.tile([P, PACK, T], F32, name="y_all")
 
-        def next_bank(name):
-            order = (0, 1, 2, 7, 3, 4, 5, 6)
-            banks_used.append(name)
-            return bank(order[(len(banks_used) - 1) % 8], name)
-
-        def look_up(c, rows):
-            tokens = slice(c * CHUNK, (c + 1) * CHUNK)
-            entries = slice(c * CHUNK // 16, (c + 1) * CHUNK // 16)
-            n = len(rows)
-            key = "%d_%d" % (c, rows[0])
-            chosen = keep.tile([P, n, CHUNK], F32, name="chosen" + key)
-            other = keep.tile([P, n, CHUNK], F32, name="other" + key)
-            gap = next_bank("gap" + key)
-            for i, j in enumerate(rows):
-                nc.vector.tensor_tensor(chosen[:, i, :], z[j][:].indirect(first[:, entries]), gate[:, tokens], ALU.mult)
-                nc.vector.tensor_tensor(other[:, i, :], z[j][:].indirect(second[:, entries]), minus_gate[:, tokens], ALU.mult)
-                nc.tensor.matmul(gap[:, i, :], chosen[:, i, :], identity[:], is_transpose=True, start=True, stop=False)
-                nc.tensor.matmul(gap[:, i, :], other[:, i, :], identity[:], is_transpose=True, start=False, stop=True)
-            size = keep.tile([P, n, CHUNK], F32, name="size" + key)
-            root = keep.tile([P, n, CHUNK], F32, name="root" + key)
-            trust = keep.tile([P, n, CHUNK], F32, name="trust" + key)
-            nc.scalar.activation(size[:], gap[:, 0:n, :], ACT.Abs, scale=inverse[:, c : c + 1])
-            nc.scalar.activation(root[:], size[:], ACT.Abs_reciprocal_sqrt, bias=one[:])
-            nc.scalar.activation(trust[:], root[:], ACT.Square)
-            back = next_bank("back" + key)
+        def look_up(u, j, t0, width):
+            tokens = slice(t0, t0 + width)
+            entries = slice(t0 // 16, (t0 + width) // 16)
+            n = width // CHUNK
+            chosen = keep.tile([P, width], F32, name="chosen%d" % u)
+            other = keep.tile([P, width], F32, name="other%d" % u)
+            gap = bank((5, 0)[u % 2], "gap%d" % u)
+            nc.vector.tensor_tensor(chosen[:], z[j][:].indirect(first[:, entries]), gate[:, tokens], ALU.mult)
+            nc.vector.tensor_tensor(other[:], z[j][:].indirect(second[:, entries]), minus_gate[:, tokens], ALU.mult)
+            for side, values in enumerate((chosen, other)):
+                for i in range(n):
+                    nc.tensor.matmul(
+                        gap[:, i, :],
+                        values[:, i * CHUNK : (i + 1) * CHUNK],
+                        identity[:],
+                        is_transpose=True,
+                        start=(side == 0 and i == 0),
+                        stop=(side == 1 and i == n - 1),
+                    )
+            part = 2
+            lanes = range(t0 // HALF, (t0 + width) // HALF)
+            size, root, trust = [], [], []
+            for s in lanes:
+                name = "%d_%d" % (j, s)
+                size.append(keep.tile([P, part, CHUNK], F32, name="size" + name, tag="stage%d_%d" % (j % 2, s), align_bytes=64))
+                root.append(keep.tile([P, part, CHUNK], F32, name="root" + name, tag="stage%d_%d" % ((j + 1) % 2, s), align_bytes=64))
+                trust.append(keep.tile([P, part, CHUNK], F32, name="trust" + name))
             for i in range(n):
-                nc.tensor.transpose(back[:, i, :], trust[:, i, :], identity[:])
-            made[(c, rows)] = (chosen, back)
+                c = t0 // CHUNK + i
+                nc.scalar.activation(size[i // part][:, i % part, :], gap[:, i, :], ACT.Abs, scale=inverse[:, c : c + 1])
+            for s in range(len(lanes)):
+                nc.scalar.activation(root[s][:], size[s][:], ACT.Abs_reciprocal_sqrt, bias=one[:])
+            for s in range(len(lanes)):
+                nc.scalar.activation(trust[s][:], root[s][:], ACT.Square)
+            back = bank((6, 7, 2, 3, 4)[u], "back%d" % u)
+            for i in range(n):
+                nc.tensor.transpose(back[:, i, :], trust[i // part][:, i % part, :], identity[:])
+            made[u] = (chosen, back)
 
-        y = [keep.tile([P, PACK, CHUNK], F32, name="y%d" % c) for c in range(CHUNKS)]
-        grouped = [keep.tile([P, CHUNK * PACK], BF16, name="y_bf%d" % c, align_bytes=64) for c in range(CHUNKS)]
+        def weigh(u, j, t0, width):
+            chosen, back = made[u]
+            tokens = slice(t0, t0 + width)
+            nc.vector.tensor_tensor(y_all[:, j, tokens], back[:].rearrange("p c t -> p (c t)")[:, :width], chosen[:], ALU.mult)
+            nc.sync.dma_start(out_rows[:, j, tokens], y_all[:, j, tokens])
 
-        def weigh(c, rows):
-            chosen, back = made[(c, rows)]
-            nc.vector.tensor_tensor(y[c][:, rows[0] : rows[-1] + 1, :], back[:, 0 : len(rows), :], chosen[:], ALU.mult)
-
-        def finish(c):
-            nc.sync.dma_start(out_rows[:, :, c * CHUNK : (c + 1) * CHUNK], y[c][:])
-            dst = grouped[c][:].rearrange("p (c i j) -> p c j i", i=4, j=PACK)
-            src = y[c][:].rearrange("p j (c i) -> p c j i", i=4)
-            if c == CHUNKS - 1:
-                nc.vector.tensor_copy(dst, src)
+        def pack(h, on_vector, tag):
+            tokens = slice(h * HALF, (h + 1) * HALF)
+            grouped = keep.tile([P, HALF * PACK], BF16, name="y_bf%d" % h, tag=tag, align_bytes=64)
+            dst = grouped[:].rearrange("p (c i j) -> p c j i", i=4, j=PACK)
+            src = y_all[:, :, tokens].rearrange("p j (c i) -> p c j i", i=4)
+            cut = on_vector // 4
+            if on_vector > 0:
+                nc.vector.tensor_copy(dst[:, :cut], src[:, :cut])
             else:
                 nc.scalar.copy(dst, src)
+            return grouped
 
-        def pack(c):
-            cols = slice(c * CHUNK, (c + 1) * CHUNK)
-            nc.vector.quantize_mx(out=y_codes[:, cols].bitcast(FP8X4), scales=y_scales[:, cols], in_=grouped[c][:])
+        def quantize_y(h, grouped):
+            tokens = slice(h * HALF, (h + 1) * HALF)
+            nc.vector.quantize_mx(out=y_codes[:, tokens].bitcast(FP8X4), scales=y_scales[:, tokens], in_=grouped[:])
+            nc.sync.dma_start(out_words[:, tokens], y_codes[:, tokens].bitcast(I32))
 
-        whole, low, high = (0, 1, 2, 3), (0, 1), (2, 3)
-        look_up(0, whole)
-        look_up(1, whole)
-        look_up(2, whole)
-        weigh(0, whole)
-        finish(0)
-        look_up(3, low)
-        look_up(3, high)
-        weigh(1, whole)
-        finish(1)
-        pack(0)
-        weigh(2, whole)
-        finish(2)
-        pack(1)
-        weigh(3, low)
-        pack(2)
-        done = (CHUNKS - 1) * CHUNK
-        nc.sync.dma_start(out_words[:, :done], y_codes[:, :done].bitcast(I32))
-        weigh(3, high)
-        finish(3)
-        pack(3)
-        nc.sync.dma_start(out_words[:, done:], y_codes[:, done:].bitcast(I32))
+        units = ((0, 0, T), (1, 0, T), (2, 0, T), (3, 0, HALF), (3, HALF, HALF))
+        for u, unit_rows in enumerate(units):
+            look_up(u, *unit_rows)
+        for u in range(4):
+            weigh(u, *units[u])
+        low = pack(0, 0, "stage0_1")
+        weigh(4, *units[4])
+        high = pack(1, HALF, "y_bf_high")
+        quantize_y(1, high)
+        quantize_y(0, low)
         for q in range(4):
             queue = nc.scalar if q % 2 == 0 else nc.sync
             queue.dma_start(out_2[0].bitcast(I32)[4 * q : 4 * q + 4, :], y_scales[32 * q : 32 * q + 4, :].bitcast(I32))

@@ -23,11 +23,10 @@ PASSES = K // (P * PACK)
 QUARTER = 128
 
 X_PIECES = ((0, 0, 256, 160), (1, 0, 256, 160), (0, 256, 256, 256), (1, 256, 128, 128), (1, 384, 128, 128))
-SPARE = 32
+SPARE = 192
 CHUNK = 128
 CHUNKS = T // CHUNK
 HALF = T // 2
-LARGEST = 3.0e38
 
 
 def tile_moe_buffer_read_with_doubt_pl_kernel(tc, xb, wa_words, wa_scales, ga, offs, offs2, out_0, out_1, out_2):
@@ -53,6 +52,11 @@ def tile_moe_buffer_read_with_doubt_pl_kernel(tc, xb, wa_words, wa_scales, ga, o
             nc.sync.dma_start(raw[:], x_rows[g][:, :, s0 : s0 + width])
             x_raw.append(raw)
 
+        table = [keep.tile([P, 2 * S + SPARE], F32, name="table%d" % j) for j in range(PACK)]
+        minus_z = [table[j][:, :S] for j in range(PACK)]
+        z = [table[j][:, S : 2 * S] for j in range(PACK)]
+        for j in range(PACK):
+            nc.gpsimd.memset(table[j][:, 2 * S :], 0.0)
         identity = keep.tile([P, P], F32, name="identity")
         make_identity(nc, identity[:])
 
@@ -60,9 +64,6 @@ def tile_moe_buffer_read_with_doubt_pl_kernel(tc, xb, wa_words, wa_scales, ga, o
             return psum.tile([P, PACK, P], F32, name=name, tag="bank%d" % b)
 
         load_x(0)
-        ga_cols = keep.tile([P, CHUNKS], F32, name="ga_cols")
-        with nc.allow_non_contiguous_dma(reason="one gate value for each partition and block of tokens"):
-            nc.sync.dma_start(ga_cols[:], ga[0].rearrange("(c p) -> p c", p=CHUNK))
         nc.sync.dma_start(
             w_raw[:].bitcast(I32).rearrange("p (g b) -> p g b", g=PASSES),
             wa_words.bitcast(I32).rearrange("g p b -> p g b"),
@@ -78,21 +79,11 @@ def tile_moe_buffer_read_with_doubt_pl_kernel(tc, xb, wa_words, wa_scales, ga, o
         second = keep.tile([P, T // 16], U16, name="second")
         nc.sync.dma_start(first[:], offs)
         nc.sync.dma_start(second[:], offs2)
+        ga_cols = keep.tile([P, CHUNKS], F32, name="ga_cols")
+        with nc.allow_non_contiguous_dma(reason="one gate value for each partition and block of tokens"):
+            nc.sync.dma_start(ga_cols[:], ga[0].rearrange("(c p) -> p c", p=CHUNK))
 
         sum_banks = (0, 2, 3, 4)
-        gate = keep.tile([P, T], F32, name="gate")
-        minus_gate = keep.tile([P, T], F32, name="minus_gate")
-        for c in range(CHUNKS):
-            spread = bank(sum_banks[c], "spread%d" % c)
-            nc.tensor.transpose(spread[:, 0, :], ga_cols[:, c : c + 1].to_broadcast([P, P]), identity[:])
-            nc.scalar.copy(gate[:, c * CHUNK : (c + 1) * CHUNK], spread[:, 0, :])
-        nc.scalar.activation(minus_gate[:], gate[:], ACT.Copy, scale=-1.0)
-        nonzero = keep.tile([P, CHUNKS], F32, name="nonzero")
-        inverse_raw = keep.tile([P, CHUNKS], F32, name="inverse_raw")
-        inverse = keep.tile([P, CHUNKS], F32, name="inverse")
-        nc.vector.scalar_tensor_tensor(nonzero[:], ga_cols[:], 0.0, ga_cols[:], ALU.is_equal, ALU.add)
-        nc.vector.reciprocal(inverse_raw[:], nonzero[:])
-        nc.vector.tensor_scalar(inverse[:], inverse_raw[:], LARGEST, -LARGEST, ALU.min, ALU.max)
 
         w = keep.tile([P, PASSES * 2 * N], U8, name="w", align_bytes=64)
         ws = keep.tile([P, PASSES * N], U8, name="ws", align_bytes=64)
@@ -136,9 +127,6 @@ def tile_moe_buffer_read_with_doubt_pl_kernel(tc, xb, wa_words, wa_scales, ga, o
                 stop=(g == PASSES - 1),
             )
 
-        z = [keep.tile([P, S + SPARE], F32, name="z%d" % j) for j in range(PACK)]
-        for j in range(PACK):
-            nc.gpsimd.memset(z[j][:, S:], 0.0)
         last = S // QUARTER - 1
         sums = [bank(sum_banks[j], "sums%d" % j) for j in range(PACK)]
         last_sums = bank(1, "last_sums")
@@ -160,6 +148,7 @@ def tile_moe_buffer_read_with_doubt_pl_kernel(tc, xb, wa_words, wa_scales, ga, o
         quantize_x(4)
         product(last_sums[:, 0, :], 0, last, 1)
         nc.scalar.copy(z[0][:, last * QUARTER : S], last_sums[:, 0, :])
+        nc.scalar.activation(minus_z[0], z[0], ACT.Copy, scale=-1.0)
         for j in range(1, PACK):
             for quarter in (0, 1):
                 products(quarter, (j,))
@@ -179,14 +168,15 @@ def tile_moe_buffer_read_with_doubt_pl_kernel(tc, xb, wa_words, wa_scales, ga, o
         y_all = keep.tile([P, PACK, T], F32, name="y_all")
 
         def look_up(u, j, t0, width):
-            tokens = slice(t0, t0 + width)
             entries = slice(t0 // 16, (t0 + width) // 16)
             n = width // CHUNK
             chosen = keep.tile([P, width], F32, name="chosen%d" % u)
             other = keep.tile([P, width], F32, name="other%d" % u)
             gap = bank((5, 0)[u % 2], "gap%d" % u)
-            nc.vector.tensor_tensor(chosen[:], z[j][:].indirect(first[:, entries]), gate[:, tokens], ALU.mult)
-            nc.vector.tensor_tensor(other[:], z[j][:].indirect(second[:, entries]), minus_gate[:, tokens], ALU.mult)
+            if j > 0 and t0 == 0:
+                nc.vector.tensor_scalar(minus_z[j], z[j], -1.0, None, ALU.mult)
+            nc.vector.tensor_copy(chosen[:], table[j][:, S:].indirect(first[:, entries]))
+            nc.vector.tensor_copy(other[:], table[j][:, : S + SPARE].indirect(second[:, entries]))
             for side, values in enumerate((chosen, other)):
                 for i in range(n):
                     nc.tensor.matmul(
@@ -199,19 +189,21 @@ def tile_moe_buffer_read_with_doubt_pl_kernel(tc, xb, wa_words, wa_scales, ga, o
                     )
             part = 2
             lanes = range(t0 // HALF, (t0 + width) // HALF)
-            size, root, trust = [], [], []
-            for s in lanes:
-                name = "%d_%d" % (j, s)
-                size.append(keep.tile([P, part, CHUNK], F32, name="size" + name, tag="stage%d_%d" % (j % 2, s), align_bytes=64))
-                root.append(keep.tile([P, part, CHUNK], F32, name="root" + name, tag="stage%d_%d" % ((j + 1) % 2, s), align_bytes=64))
-                trust.append(keep.tile([P, part, CHUNK], F32, name="trust" + name))
-            for i in range(n):
-                c = t0 // CHUNK + i
-                nc.scalar.activation(size[i // part][:, i % part, :], gap[:, i, :], ACT.Abs, scale=inverse[:, c : c + 1])
-            for s in range(len(lanes)):
-                nc.scalar.activation(root[s][:], size[s][:], ACT.Abs_reciprocal_sqrt, bias=one[:])
-            for s in range(len(lanes)):
-                nc.scalar.activation(trust[s][:], root[s][:], ACT.Square)
+            size, root, square, trust = [], [], [], []
+            for k, s in enumerate(lanes):
+                size.append(keep.tile([P, part, CHUNK], F32, name="size%d_%d" % (j, s), tag="ends%d" % s, align_bytes=64))
+                nc.scalar.activation(size[k][:], gap[:, k * part : (k + 1) * part, :], ACT.Abs)
+            for k, s in enumerate(lanes):
+                root.append(keep.tile([P, part, CHUNK], F32, name="root%d_%d" % (j, s), tag="middle%d" % s))
+                nc.scalar.activation(root[k][:], size[k][:], ACT.Abs_reciprocal_sqrt, bias=one[:])
+            for k, s in enumerate(lanes):
+                square.append(keep.tile([P, part, CHUNK], F32, name="square%d_%d" % (j, s), tag="ends%d" % s, align_bytes=64))
+                nc.scalar.activation(square[k][:], root[k][:], ACT.Square)
+            for k, s in enumerate(lanes):
+                trust.append(keep.tile([P, part, CHUNK], F32, name="trust%d_%d" % (j, s)))
+                for i in range(part):
+                    c = s * part + i
+                    nc.scalar.activation(trust[k][:, i, :], square[k][:, i, :], ACT.Copy, scale=ga_cols[:, c : c + 1])
             back = bank((6, 7, 2, 3, 4)[u], "back%d" % u)
             for i in range(n):
                 nc.tensor.transpose(back[:, i, :], trust[i // part][:, i % part, :], identity[:])
@@ -245,7 +237,7 @@ def tile_moe_buffer_read_with_doubt_pl_kernel(tc, xb, wa_words, wa_scales, ga, o
             look_up(u, *unit_rows)
         for u in range(4):
             weigh(u, *units[u])
-        low = pack(0, 0, "stage0_1")
+        low = pack(0, 0, "ends1")
         weigh(4, *units[4])
         high = pack(1, HALF, "y_bf_high")
         quantize_y(1, high)

from contextlib import ExitStack

import concourse.mybir as mybir
from concourse.masks import make_identity

K, S, T, N = 1024, 512, 512, 512
FLOPS = 2 * K * S * N

F32 = mybir.dt.float32
BF16 = mybir.dt.bfloat16
I32 = mybir.dt.int32
U32 = mybir.dt.uint32
U16 = mybir.dt.uint16
U8 = mybir.dt.uint8
FP8X4 = mybir.dt.float8_e4m3fn_x4
FP4X4 = mybir.dt.float4_e2m1fn_x4
ALU = mybir.AluOpType
ACT = mybir.ActivationFunctionType

P = 128
PACK = 4
PASSES = K // (P * PACK)
QUARTER = 128

X_PIECES = ((0, 0, 256, 160), (1, 0, 256, 160), (0, 256, 256, 256), (1, 256, 128, 128), (1, 384, 128, 128))
SPARE = 192
CHUNK = 128
CHUNKS = T // CHUNK
HALF = T // 2


def tile_moe_buffer_read_with_doubt_pl_kernel(tc, xb, wa_words, wa_scales, ga, offs, offs2, out_0, out_1, out_2):
    nc = tc.nc
    with ExitStack() as ctx:
        keep = ctx.enter_context(tc.tile_pool(name="keep", bufs=1))
        psum = ctx.enter_context(tc.psum_pool(name="psum", bufs=1))

        w_raw = keep.tile([P, PASSES * 2 * N], U8, name="w_raw", align_bytes=64)
        ws_raw = keep.tile([P, PASSES * N], U8, name="ws_raw", align_bytes=64)
        nc.gpsimd.memset(ws_raw[:].bitcast(I32), 0)
        unit = keep.tile([P, 1], F32, name="unit")
        one = keep.tile([P, 1], F32, name="one")
        nc.gpsimd.memset(unit[:], 1.0)
        nc.scalar.activation(one[:], unit[:], ACT.Abs_reciprocal_sqrt)

        x_rows = xb.rearrange("(g p j) s -> g p j s", g=PASSES, j=PACK)
        x_raw = []

        def load_x(i):
            g, s0, width, on_vector = X_PIECES[i]
            raw = keep.tile([P, PACK, width], F32, name="x_raw%d" % i)
            nc.sync.dma_start(raw[:], x_rows[g][:, :, s0 : s0 + width])
            x_raw.append(raw)

        table = [keep.tile([P, 2 * S + SPARE], F32, name="table%d" % j) for j in range(PACK)]
        minus_z = [table[j][:, :S] for j in range(PACK)]
        z = [table[j][:, S : 2 * S] for j in range(PACK)]
        for j in range(PACK):
            nc.gpsimd.memset(table[j][:, 2 * S :], 0.0)
        identity = keep.tile([P, P], F32, name="identity")
        make_identity(nc, identity[:])

        def bank(b, name):
            return psum.tile([P, PACK, P], F32, name=name, tag="bank%d" % b)

        load_x(0)
        nc.sync.dma_start(
            w_raw[:].bitcast(I32).rearrange("p (g b) -> p g b", g=PASSES),
            wa_words.bitcast(I32).rearrange("g p b -> p g b"),
        )
        for q in range(4):
            nc.sync.dma_start(
                ws_raw[32 * q : 32 * q + 4, :].bitcast(I32).rearrange("p (g b) -> p g b", g=PASSES),
                wa_scales.bitcast(I32).rearrange("g r b -> r g b")[4 * q : 4 * q + 4],
            )
        for i in range(1, len(X_PIECES)):
            load_x(i)
        first = keep.tile([P, T // 16], U16, name="first")
        second = keep.tile([P, T // 16], U16, name="second")
        nc.sync.dma_start(first[:], offs)
        nc.sync.dma_start(second[:], offs2)
        ga_cols = keep.tile([P, CHUNKS], F32, name="ga_cols")
        with nc.allow_non_contiguous_dma(reason="one gate value for each partition and block of tokens"):
            nc.sync.dma_start(ga_cols[:], ga[0].rearrange("(c p) -> p c", p=CHUNK))

        sum_banks = (0, 2, 3, 4)

        w = keep.tile([P, PASSES * 2 * N], U8, name="w", align_bytes=64)
        ws = keep.tile([P, PASSES * N], U8, name="ws", align_bytes=64)
        nc.vector.tensor_copy(
            w[:].bitcast(U16).rearrange("p (g j m) -> p g j m", g=PASSES, j=PACK),
            w_raw[:].bitcast(U16).rearrange("p (g m j) -> p g j m", g=PASSES, j=PACK),
        )
        nc.vector.tensor_copy(
            ws[:].rearrange("p (g j m) -> p g j m", g=PASSES, j=PACK),
            ws_raw[:].rearrange("p (g m j) -> p g j m", g=PASSES, j=PACK),
        )

        x_codes = {}

        def quantize_x(i):
            g, s0, width, on_vector = X_PIECES[i]
            grouped = keep.tile([P, width * PACK], BF16, name="x_bf%d" % i, align_bytes=64)
            dst = grouped[:].rearrange("p (c i j) -> p c j i", i=4, j=PACK)
            src = x_raw[i][:].rearrange("p j (c i) -> p c j i", i=4)
            cut = on_vector // 4
            if on_vector < width:
                nc.scalar.copy(dst[:, cut:], src[:, cut:])
            nc.vector.tensor_copy(dst[:, :cut], src[:, :cut])
            codes = keep.tile([P, width], U32, name="x_codes%d" % i, align_bytes=64)
            scales = keep.tile([P, width], U8, name="x_scales%d" % i, align_bytes=64)
            nc.vector.quantize_mx(out=codes[:].bitcast(FP8X4), scales=scales[:], in_=grouped[:])
            for a in range(width // QUARTER):
                cols = slice(a * QUARTER, (a + 1) * QUARTER)
                x_codes[(g, s0 // QUARTER + a)] = (codes[:, cols], scales[:, cols])

        def product(out, j, quarter, g):
            codes, scales = x_codes[(g, quarter)]
            block = g * PACK + j
            nc.tensor.matmul_mx(
                out=out,
                lhsT=w[:, block * 2 * P : (block + 1) * 2 * P].bitcast(FP4X4),
                lhsT_scale=ws[:, block * P : (block + 1) * P],
                rhs=codes.bitcast(FP8X4),
                rhs_scale=scales,
                start=(g == 0),
                stop=(g == PASSES - 1),
            )

        last = S // QUARTER - 1
        sums = [bank(sum_banks[j], "sums%d" % j) for j in range(PACK)]
        last_sums = bank(1, "last_sums")

        def products(quarter, rows):
            for j in rows:
                for g in range(PASSES):
                    product(sums[j][:, quarter, :], j, quarter, g)

        quantize_x(0)
        quantize_x(1)
        products(0, (0,))
        products(1, (0,))
        quantize_x(2)
        product(last_sums[:, 0, :], 0, last, 0)
        quantize_x(3)
        products(2, (0,))
        nc.scalar.copy(z[0][:, : last * QUARTER], sums[0][:, 0:last, :].rearrange("p q s -> p (q s)"))
        quantize_x(4)
        product(last_sums[:, 0, :], 0, last, 1)
        nc.scalar.copy(z[0][:, last * QUARTER : S], last_sums[:, 0, :])
        nc.scalar.activation(minus_z[0], z[0], ACT.Copy, scale=-1.0)
        for j in range(1, PACK):
            for quarter in (0, 1):
                products(quarter, (j,))
            late_sums = bank(1, "late_sums%d" % j)
            for quarter in (2, 3):
                for g in range(PASSES):
                    product(late_sums[:, quarter, :], j, quarter, g)
            nc.scalar.copy(z[j][:, : S // 2], sums[j][:, 0:2, :].rearrange("p q s -> p (q s)"))
            nc.scalar.copy(z[j][:, S // 2 : S], late_sums[:, 2:4, :].rearrange("p q s -> p (q s)"))

        y_codes = keep.tile([P, T], U32, name="y_codes", align_bytes=64)
        y_scales = keep.tile([P, T], U8, name="y_scales", align_bytes=64)
        out_rows = out_0.rearrange("(p j) t -> p j t", j=PACK)
        out_words = out_1[0].rearrange("p c r -> p (c r)").bitcast(I32)
        made = {}

        y_all = keep.tile([P, PACK, T], F32, name="y_all")

        def look_up(u, j, t0, width):
            entries = slice(t0 // 16, (t0 + width) // 16)
            n = width // CHUNK
            chosen = keep.tile([P, width], F32, name="chosen%d" % u)
            other = keep.tile([P, width], F32, name="other%d" % u)
            gap = bank((5, 0)[u % 2], "gap%d" % u)
            if j > 0 and t0 == 0:
                nc.vector.tensor_scalar(minus_z[j], z[j], -1.0, None, ALU.mult)
            nc.vector.tensor_copy(chosen[:], table[j][:, S:].indirect(first[:, entries]))
            nc.vector.tensor_copy(other[:], table[j][:, : S + SPARE].indirect(second[:, entries]))
            for side, values in enumerate((chosen, other)):
                for i in range(n):
                    nc.tensor.matmul(
                        gap[:, i, :],
                        values[:, i * CHUNK : (i + 1) * CHUNK],
                        identity[:],
                        is_transpose=True,
                        start=(side == 0 and i == 0),
                        stop=(side == 1 and i == n - 1),
                    )
            part = 2
            lanes = range(t0 // HALF, (t0 + width) // HALF)
            size, root, square, trust = [], [], [], []
            for k, s in enumerate(lanes):
                size.append(keep.tile([P, part, CHUNK], F32, name="size%d_%d" % (j, s), tag="ends%d" % s, align_bytes=64))
                nc.scalar.activation(size[k][:], gap[:, k * part : (k + 1) * part, :], ACT.Abs)
            for k, s in enumerate(lanes):
                root.append(keep.tile([P, part, CHUNK], F32, name="root%d_%d" % (j, s), tag="middle%d" % s))
                nc.scalar.activation(root[k][:], size[k][:], ACT.Abs_reciprocal_sqrt, bias=one[:])
            for k, s in enumerate(lanes):
                square.append(keep.tile([P, part, CHUNK], F32, name="square%d_%d" % (j, s), tag="ends%d" % s, align_bytes=64))
                nc.scalar.activation(square[k][:], root[k][:], ACT.Square)
            for k, s in enumerate(lanes):
                trust.append(keep.tile([P, part, CHUNK], F32, name="trust%d_%d" % (j, s)))
                for i in range(part):
                    c = s * part + i
                    nc.scalar.activation(trust[k][:, i, :], square[k][:, i, :], ACT.Copy, scale=ga_cols[:, c : c + 1])
            back = bank((6, 7, 2, 3, 4)[u], "back%d" % u)
            for i in range(n):
                nc.tensor.transpose(back[:, i, :], trust[i // part][:, i % part, :], identity[:])
            made[u] = (chosen, back)

        def weigh(u, j, t0, width):
            chosen, back = made[u]
            tokens = slice(t0, t0 + width)
            nc.vector.tensor_tensor(y_all[:, j, tokens], back[:].rearrange("p c t -> p (c t)")[:, :width], chosen[:], ALU.mult)
            nc.sync.dma_start(out_rows[:, j, tokens], y_all[:, j, tokens])

        def pack(h, on_vector, tag):
            tokens = slice(h * HALF, (h + 1) * HALF)
            grouped = keep.tile([P, HALF * PACK], BF16, name="y_bf%d" % h, tag=tag, align_bytes=64)
            dst = grouped[:].rearrange("p (c i j) -> p c j i", i=4, j=PACK)
            src = y_all[:, :, tokens].rearrange("p j (c i) -> p c j i", i=4)
            cut = on_vector // 4
            if on_vector > 0:
                nc.vector.tensor_copy(dst[:, :cut], src[:, :cut])
            else:
                nc.scalar.copy(dst, src)
            return grouped

        def quantize_y(h, grouped):
            tokens = slice(h * HALF, (h + 1) * HALF)
            nc.vector.quantize_mx(out=y_codes[:, tokens].bitcast(FP8X4), scales=y_scales[:, tokens], in_=grouped[:])
            nc.sync.dma_start(out_words[:, tokens], y_codes[:, tokens].bitcast(I32))

        units = ((0, 0, T), (1, 0, T), (2, 0, T), (3, 0, HALF), (3, HALF, HALF))
        for u, unit_rows in enumerate(units):
            look_up(u, *unit_rows)
        for u in range(4):
            weigh(u, *units[u])
        low = pack(0, 0, "ends1")
        weigh(4, *units[4])
        high = pack(1, HALF, "y_bf_high")
        quantize_y(1, high)
        quantize_y(0, low)
        for q in range(4):
            queue = nc.scalar if q % 2 == 0 else nc.sync
            queue.dma_start(out_2[0].bitcast(I32)[4 * q : 4 * q + 4, :], y_scales[32 * q : 32 * q + 4, :].bitcast(I32))
